import numpy as np
import ml_dtypes

BF16 = ml_dtypes.bfloat16


def bf(x):
    return np.asarray(x, np.float32).astype(BF16)


def f32(x):
    return np.asarray(x, np.float32)


def f64(x):
    return np.asarray(x).astype(np.float64)


def striped(idx):
    return np.concatenate([l.reshape(-1, 16).T for l in idx])


def rows(idx, k):
    return np.tile(np.repeat(idx, 16, axis=0), (k // (16 * 8), 1))


def look(tab, idx):
    return np.take_along_axis(f64(tab), rows(idx, len(tab)), axis=1)


K, S, H, D, V, N, M = 128, 2048, 256, 2, 512, 1024, 256


def setup_inputs():
    return {"z": bf(np.random.standard_normal((H, S))), "wt": bf(np.random.standard_normal((H, K)) / np.sqrt(H)), "x0": f32(1.0 * np.random.standard_normal((K, V))), "w": bf(np.random.standard_normal((K, M)) / np.sqrt(K)), "b": f32(0.5 * np.random.standard_normal((M, 1))), "offs": striped(np.stack([np.random.permutation(S)[:N] for _ in range(8)]))}


def reference(z, wt, x0, w, b, offs):
    idx = np.stack([g.T.reshape(-1) for g in np.split(offs, 8)])
    tab = f64(wt).T @ f64(z)
    x = f64(x0)
    for d in range(D):
        x = np.maximum(x, look(tab, idx[:, d * V:(d + 1) * V]))
    return np.maximum(f64(w).T @ x + f64(b), 0.0)

@@ -1,0 +1,78 @@
+import concourse.mybir as mybir
+
+BF16, F32, U16 = mybir.dt.bfloat16, mybir.dt.float32, mybir.dt.uint16
+ALU = mybir.AluOpType
+ACT = mybir.ActivationFunctionType
+
+P = 128
+BANK = 512
+GROUP = 16
+
+FLOPS = 2 * 256 * 128 * 2048 + 2 * 128 * 256 * 512
+
+
+def tile_lookup_pjmax_relu_kernel(tc, z, wt, x0, w, b, offs, out):
+    nc = tc.nc
+    features, places = z.shape
+    nodes = x0.shape[1]
+    outputs = w.shape[1]
+    k_blocks = features // P
+    m_blocks = outputs // P
+    chunks = places // BANK
+    neighbours = offs.shape[1] * GROUP // nodes
+    piece_cols = nodes // GROUP
+
+    z_rows = z.rearrange("(p c) i -> p c i", c=k_blocks)
+    wt_rows = wt.rearrange("(p c) r -> p c r", c=k_blocks)
+    b_rows = b.rearrange("(p c) o -> p (c o)", c=m_blocks)
+    out_rows = out.rearrange("(p c) j -> p c j", c=m_blocks)
+
+    with (
+        tc.tile_pool(name="held", bufs=1) as held,
+        tc.psum_pool(name="psum", bufs=1) as psum,
+    ):
+        offsets = held.tile([P, offs.shape[1]], U16, name="offsets")
+        wt_sb = held.tile([P, k_blocks, P], BF16, name="wt_sb")
+        z_sb = [held.tile([P, k_blocks, BANK], BF16, name=f"z_sb{q}") for q in range(chunks)]
+        x0_sb = held.tile([P, nodes], F32, name="x0_sb")
+        w_sb = held.tile([P, outputs], BF16, name="w_sb")
+        b_sb = held.tile([P, m_blocks], F32, name="b_sb")
+        table = held.tile([P, places], F32, name="table")
+
+        nc.scalar.dma_start(wt_sb[:], wt_rows)
+        for q in range(chunks):
+            nc.sync.dma_start(z_sb[q][:], z_rows[:, :, q * BANK:(q + 1) * BANK])
+        nc.sync.dma_start(offsets[:], offs)
+        nc.sync.dma_start(x0_sb[:], x0)
+        nc.gpsimd.dma_start(w_sb[:], w)
+        nc.gpsimd.dma_start(b_sb[:], b_rows)
+
+        for q in range(chunks):
+            projected = psum.tile([P, BANK], F32, name=f"projected{q}")
+            for c in range(k_blocks):
+                nc.tensor.matmul(projected[:], wt_sb[:, c, :], z_sb[q][:, c, :],
+                                 start=(c == 0), stop=(c == k_blocks - 1))
+            if q % 2 == 0:
+                nc.scalar.copy(table[:, q * BANK:(q + 1) * BANK], projected[:])
+            else:
+                nc.vector.tensor_copy(table[:, q * BANK:(q + 1) * BANK], projected[:])
+
+        running = x0_sb
+        for d in range(neighbours):
+            larger = held.tile([P, nodes], F32, name=f"larger{d}")
+            piece = offsets[:, d * piece_cols:(d + 1) * piece_cols]
+            nc.vector.tensor_tensor(larger[:], table[:].indirect(piece), running[:], ALU.max)
+            running = larger
+        x_bf = held.tile([P, nodes], BF16, name="x_bf")
+        nc.vector.tensor_copy(x_bf[:], running[:])
+
+        w_cols = w_sb[:].rearrange("r (m c) -> r c m", c=m_blocks)
+        for c in range(m_blocks):
+            product = psum.tile([P, nodes], F32, name=f"product{c}")
+            result = held.tile([P, nodes], F32, name=f"result{c}")
+            nc.tensor.matmul(product[:], w_cols[:, c, :], x_bf[:], start=True, stop=True)
+            if c % 2 == 0:
+                nc.scalar.activation(result[:], product[:], ACT.Relu, bias=b_sb[:, c:c + 1])
+            else:
+                nc.vector.tensor_scalar(result[:], product[:], b_sb[:, c:c + 1], 0.0, ALU.add, ALU.max)
+            nc.sync.dma_start(out_rows[:, c, :], result[:])

@@ -5,8 +5,13 @@ ALU = mybir.AluOpType
 ACT = mybir.ActivationFunctionType
 
 P = 128
+PSUM_BANKS = 8
 BANK = 512
+STRIP = 256
+LOAD = 1024
 GROUP = 16
+WARM_UP = 10
+KEEP_WARM = 12
 
 FLOPS = 2 * 256 * 128 * 2048 + 2 * 128 * 256 * 512
 
@@ -18,7 +23,6 @@ def tile_lookup_pjmax_relu_kernel(tc, z, wt, x0, w, b, offs, out):
     outputs = w.shape[1]
     k_blocks = features // P
     m_blocks = outputs // P
-    chunks = places // BANK
     neighbours = offs.shape[1] * GROUP // nodes
     piece_cols = nodes // GROUP
 
@@ -29,33 +33,49 @@ def tile_lookup_pjmax_relu_kernel(tc, z, wt, x0, w, b, offs, out):
 
     with (
         tc.tile_pool(name="held", bufs=1) as held,
-        tc.psum_pool(name="psum", bufs=1) as psum,
+        tc.psum_pool(name="psum", bufs=PSUM_BANKS) as psum,
     ):
         offsets = held.tile([P, offs.shape[1]], U16, name="offsets")
         wt_sb = held.tile([P, k_blocks, P], BF16, name="wt_sb")
-        z_sb = [held.tile([P, k_blocks, BANK], BF16, name=f"z_sb{q}") for q in range(chunks)]
         x0_sb = held.tile([P, nodes], F32, name="x0_sb")
         w_sb = held.tile([P, outputs], BF16, name="w_sb")
         b_sb = held.tile([P, m_blocks], F32, name="b_sb")
         table = held.tile([P, places], F32, name="table")
+        zeros = held.tile([P, STRIP], BF16, name="zeros")
 
         nc.scalar.dma_start(wt_sb[:], wt_rows)
-        for q in range(chunks):
-            nc.sync.dma_start(z_sb[q][:], z_rows[:, :, q * BANK:(q + 1) * BANK])
+        z_sb = {}
+        for h in range(places // LOAD):
+            for c in range(k_blocks):
+                z_sb[h, c] = held.tile([P, LOAD], BF16, name=f"z_sb{h}_{c}")
+                nc.sync.dma_start(z_sb[h, c][:], z_rows[:, c, h * LOAD:(h + 1) * LOAD])
         nc.sync.dma_start(offsets[:], offs)
         nc.sync.dma_start(x0_sb[:], x0)
-        nc.gpsimd.dma_start(w_sb[:], w)
-        nc.gpsimd.dma_start(b_sb[:], b_rows)
+        nc.sync.dma_start(w_sb[:], w)
+        nc.sync.dma_start(b_sb[:], b_rows)
 
-        for q in range(chunks):
-            projected = psum.tile([P, BANK], F32, name=f"projected{q}")
+        nc.vector.memset(zeros[:], 0.0)
+        unread = psum.tile([P, BANK], F32, name="unread", tag="bank")
+        for step in range(WARM_UP):
+            nc.tensor.matmul(unread[:, :STRIP], zeros[:, :P], zeros[:], start=True, stop=True)
+
+        for h in range(places // LOAD):
+            strips = [psum.tile([P, BANK], F32, name=f"projected{h}_{s}", tag="bank") for s in range(LOAD // STRIP)]
             for c in range(k_blocks):
-                nc.tensor.matmul(projected[:], wt_sb[:, c, :], z_sb[q][:, c, :],
-                                 start=(c == 0), stop=(c == k_blocks - 1))
-            if q % 2 == 0:
-                nc.scalar.copy(table[:, q * BANK:(q + 1) * BANK], projected[:])
-            else:
-                nc.vector.tensor_copy(table[:, q * BANK:(q + 1) * BANK], projected[:])
+                for s, strip in enumerate(strips):
+                    nc.tensor.matmul(strip[:, :STRIP], wt_sb[:, c, :], z_sb[h, c][:, s * STRIP:(s + 1) * STRIP],
+                                     start=(c == 0), stop=(c == k_blocks - 1))
+            for s, strip in enumerate(strips):
+                first = h * LOAD + s * STRIP
+                if s % 2 == 0:
+                    nc.scalar.copy(table[:, first:first + STRIP], strip[:, :STRIP])
+                else:
+                    nc.vector.tensor_copy(table[:, first:first + STRIP], strip[:, :STRIP])
+
+        last_z = z_sb[places // LOAD - 1, k_blocks - 1]
+        unread_again = psum.tile([P, BANK], F32, name="unread_again", tag="bank")
+        for step in range(KEEP_WARM):
+            nc.tensor.matmul(unread_again[:], wt_sb[:, k_blocks - 1, :], last_z[:, :BANK], start=True, stop=True)
 
         running = x0_sb
         for d in range(neighbours):
@@ -63,16 +83,19 @@ def tile_lookup_pjmax_relu_kernel(tc, z, wt, x0, w, b, offs, out):
             piece = offsets[:, d * piece_cols:(d + 1) * piece_cols]
             nc.vector.tensor_tensor(larger[:], table[:].indirect(piece), running[:], ALU.max)
             running = larger
-        x_bf = held.tile([P, nodes], BF16, name="x_bf")
-        nc.vector.tensor_copy(x_bf[:], running[:])
+
+        x_bf = [held.tile([P, STRIP], BF16, name=f"x_bf{s}") for s in range(nodes // STRIP)]
+        for s, x_strip in enumerate(x_bf):
+            nc.vector.tensor_copy(x_strip[:], running[:, s * STRIP:(s + 1) * STRIP])
 
         w_cols = w_sb[:].rearrange("r (m c) -> r c m", c=m_blocks)
-        for c in range(m_blocks):
-            product = psum.tile([P, nodes], F32, name=f"product{c}")
-            result = held.tile([P, nodes], F32, name=f"result{c}")
-            nc.tensor.matmul(product[:], w_cols[:, c, :], x_bf[:], start=True, stop=True)
-            if c % 2 == 0:
-                nc.scalar.activation(result[:], product[:], ACT.Relu, bias=b_sb[:, c:c + 1])
-            else:
-                nc.vector.tensor_scalar(result[:], product[:], b_sb[:, c:c + 1], 0.0, ALU.add, ALU.max)
-            nc.sync.dma_start(out_rows[:, c, :], result[:])
+        for s, x_strip in enumerate(x_bf):
+            for c in range(m_blocks):
+                product = psum.tile([P, BANK], F32, name=f"product{s}_{c}", tag="bank")
+                result = held.tile([P, STRIP], F32, name=f"result{s}_{c}")
+                nc.tensor.matmul(product[:, :STRIP], w_cols[:, c, :], x_strip[:], start=True, stop=True)
+                if c % 2 == 0:
+                    nc.scalar.activation(result[:], product[:, :STRIP], ACT.Relu, bias=b_sb[:, c:c + 1])
+                else:
+                    nc.vector.tensor_scalar(result[:], product[:, :STRIP], b_sb[:, c:c + 1], 0.0, ALU.add, ALU.max)
+                nc.sync.dma_start(out_rows[:, c, s * STRIP:(s + 1) * STRIP], result[:])

@@ -10,8 +10,8 @@ BANK = 512
 STRIP = 256
 LOAD = 1024
 GROUP = 16
-WARM_UP = 10
-KEEP_WARM = 12
+WARM_UP = 8
+KEEP_WARM = 10
 
 FLOPS = 2 * 256 * 128 * 2048 + 2 * 128 * 256 * 512
 
@@ -25,6 +25,7 @@ def tile_lookup_pjmax_relu_kernel(tc, z, wt, x0, w, b, offs, out):
     m_blocks = outputs // P
     neighbours = offs.shape[1] * GROUP // nodes
     piece_cols = nodes // GROUP
+    assert neighbours == 2
 
     z_rows = z.rearrange("(p c) i -> p c i", c=k_blocks)
     wt_rows = wt.rearrange("(p c) r -> p c r", c=k_blocks)
@@ -48,13 +49,17 @@ def tile_lookup_pjmax_relu_kernel(tc, z, wt, x0, w, b, offs, out):
         for h in range(places // LOAD):
             for c in range(k_blocks):
                 z_sb[h, c] = held.tile([P, LOAD], BF16, name=f"z_sb{h}_{c}")
-                nc.sync.dma_start(z_sb[h, c][:], z_rows[:, c, h * LOAD:(h + 1) * LOAD])
+                is_last = (h, c) == (places // LOAD - 1, k_blocks - 1)
+                width = LOAD // 2 if is_last else LOAD
+                for first in range(0, LOAD, width):
+                    nc.sync.dma_start(z_sb[h, c][:, first:first + width],
+                                      z_rows[:, c, h * LOAD + first:h * LOAD + first + width])
         nc.sync.dma_start(offsets[:], offs)
         nc.sync.dma_start(x0_sb[:], x0)
         nc.sync.dma_start(w_sb[:], w)
         nc.sync.dma_start(b_sb[:], b_rows)
 
-        nc.vector.memset(zeros[:], 0.0)
+        nc.gpsimd.memset(zeros[:], 0.0)
         unread = psum.tile([P, BANK], F32, name="unread", tag="bank")
         for step in range(WARM_UP):
             nc.tensor.matmul(unread[:, :STRIP], zeros[:, :P], zeros[:], start=True, stop=True)
@@ -75,18 +80,17 @@ def tile_lookup_pjmax_relu_kernel(tc, z, wt, x0, w, b, offs, out):
         last_z = z_sb[places // LOAD - 1, k_blocks - 1]
         unread_again = psum.tile([P, BANK], F32, name="unread_again", tag="bank")
         for step in range(KEEP_WARM):
-            nc.tensor.matmul(unread_again[:], wt_sb[:, k_blocks - 1, :], last_z[:, :BANK], start=True, stop=True)
+            nc.tensor.matmul(unread_again[:], wt_sb[:, k_blocks - 1, :], last_z[:, LOAD - BANK:], start=True, stop=True)
 
-        running = x0_sb
+        larger = [held.tile([P, nodes], F32, name=f"larger{d}") for d in range(neighbours)]
         for d in range(neighbours):
-            larger = held.tile([P, nodes], F32, name=f"larger{d}")
             piece = offsets[:, d * piece_cols:(d + 1) * piece_cols]
-            nc.vector.tensor_tensor(larger[:], table[:].indirect(piece), running[:], ALU.max)
-            running = larger
+            nc.vector.tensor_tensor(larger[d][:], table[:].indirect(piece), x0_sb[:], ALU.max)
 
         x_bf = [held.tile([P, STRIP], BF16, name=f"x_bf{s}") for s in range(nodes // STRIP)]
         for s, x_strip in enumerate(x_bf):
-            nc.vector.tensor_copy(x_strip[:], running[:, s * STRIP:(s + 1) * STRIP])
+            columns = slice(s * STRIP, (s + 1) * STRIP)
+            nc.vector.tensor_tensor(x_strip[:], larger[0][:, columns], larger[1][:, columns], ALU.max)
 
         w_cols = w_sb[:].rearrange("r (m c) -> r c m", c=m_blocks)
         for s, x_strip in enumerate(x_bf):

import concourse.mybir as mybir

BF16, F32, U16 = mybir.dt.bfloat16, mybir.dt.float32, mybir.dt.uint16
ALU = mybir.AluOpType
ACT = mybir.ActivationFunctionType

P = 128
PSUM_BANKS = 8
BANK = 512
STRIP = 256
LOAD = 1024
GROUP = 16
WARM_UP = 8
KEEP_WARM = 10

FLOPS = 2 * 256 * 128 * 2048 + 2 * 128 * 256 * 512


def tile_lookup_pjmax_relu_kernel(tc, z, wt, x0, w, b, offs, out):
    nc = tc.nc
    features, places = z.shape
    nodes = x0.shape[1]
    outputs = w.shape[1]
    k_blocks = features // P
    m_blocks = outputs // P
    neighbours = offs.shape[1] * GROUP // nodes
    piece_cols = nodes // GROUP
    assert neighbours == 2

    z_rows = z.rearrange("(p c) i -> p c i", c=k_blocks)
    wt_rows = wt.rearrange("(p c) r -> p c r", c=k_blocks)
    b_rows = b.rearrange("(p c) o -> p (c o)", c=m_blocks)
    out_rows = out.rearrange("(p c) j -> p c j", c=m_blocks)

    with (
        tc.tile_pool(name="held", bufs=1) as held,
        tc.psum_pool(name="psum", bufs=PSUM_BANKS) as psum,
    ):
        offsets = held.tile([P, offs.shape[1]], U16, name="offsets")
        wt_sb = held.tile([P, k_blocks, P], BF16, name="wt_sb")
        x0_sb = held.tile([P, nodes], F32, name="x0_sb")
        w_sb = held.tile([P, outputs], BF16, name="w_sb")
        b_sb = held.tile([P, m_blocks], F32, name="b_sb")
        table = held.tile([P, places], F32, name="table")
        zeros = held.tile([P, STRIP], BF16, name="zeros")

        nc.scalar.dma_start(wt_sb[:], wt_rows)
        z_sb = {}
        for h in range(places // LOAD):
            for c in range(k_blocks):
                z_sb[h, c] = held.tile([P, LOAD], BF16, name=f"z_sb{h}_{c}")
                is_last = (h, c) == (places // LOAD - 1, k_blocks - 1)
                width = LOAD // 2 if is_last else LOAD
                for first in range(0, LOAD, width):
                    nc.sync.dma_start(z_sb[h, c][:, first:first + width],
                                      z_rows[:, c, h * LOAD + first:h * LOAD + first + width])
        nc.sync.dma_start(offsets[:], offs)
        nc.sync.dma_start(x0_sb[:], x0)
        nc.sync.dma_start(w_sb[:], w)
        nc.sync.dma_start(b_sb[:], b_rows)

        nc.gpsimd.memset(zeros[:], 0.0)
        unread = psum.tile([P, BANK], F32, name="unread", tag="bank")
        for step in range(WARM_UP):
            nc.tensor.matmul(unread[:, :STRIP], zeros[:, :P], zeros[:], start=True, stop=True)

        for h in range(places // LOAD):
            strips = [psum.tile([P, BANK], F32, name=f"projected{h}_{s}", tag="bank") for s in range(LOAD // STRIP)]
            for c in range(k_blocks):
                for s, strip in enumerate(strips):
                    nc.tensor.matmul(strip[:, :STRIP], wt_sb[:, c, :], z_sb[h, c][:, s * STRIP:(s + 1) * STRIP],
                                     start=(c == 0), stop=(c == k_blocks - 1))
            for s, strip in enumerate(strips):
                first = h * LOAD + s * STRIP
                if s % 2 == 0:
                    nc.scalar.copy(table[:, first:first + STRIP], strip[:, :STRIP])
                else:
                    nc.vector.tensor_copy(table[:, first:first + STRIP], strip[:, :STRIP])

        last_z = z_sb[places // LOAD - 1, k_blocks - 1]
        unread_again = psum.tile([P, BANK], F32, name="unread_again", tag="bank")
        for step in range(KEEP_WARM):
            nc.tensor.matmul(unread_again[:], wt_sb[:, k_blocks - 1, :], last_z[:, LOAD - BANK:], start=True, stop=True)

        larger = [held.tile([P, nodes], F32, name=f"larger{d}") for d in range(neighbours)]
        for d in range(neighbours):
            piece = offsets[:, d * piece_cols:(d + 1) * piece_cols]
            nc.vector.tensor_tensor(larger[d][:], table[:].indirect(piece), x0_sb[:], ALU.max)

        x_bf = [held.tile([P, STRIP], BF16, name=f"x_bf{s}") for s in range(nodes // STRIP)]
        for s, x_strip in enumerate(x_bf):
            columns = slice(s * STRIP, (s + 1) * STRIP)
            nc.vector.tensor_tensor(x_strip[:], larger[0][:, columns], larger[1][:, columns], ALU.max)

        w_cols = w_sb[:].rearrange("r (m c) -> r c m", c=m_blocks)
        for s, x_strip in enumerate(x_bf):
            for c in range(m_blocks):
                product = psum.tile([P, BANK], F32, name=f"product{s}_{c}", tag="bank")
                result = held.tile([P, STRIP], F32, name=f"result{s}_{c}")
                nc.tensor.matmul(product[:, :STRIP], w_cols[:, c, :], x_strip[:], start=True, stop=True)
                if c % 2 == 0:
                    nc.scalar.activation(result[:], product[:, :STRIP], ACT.Relu, bias=b_sb[:, c:c + 1])
                else:
                    nc.vector.tensor_scalar(result[:], product[:, :STRIP], b_sb[:, c:c + 1], 0.0, ALU.add, ALU.max)
                nc.sync.dma_start(out_rows[:, c, s * STRIP:(s + 1) * STRIP], result[:])
